import numpy as np
import ml_dtypes


def mxq(x, axis, fmt="e4m3"):
    dtype, down = {"e4m3": (ml_dtypes.float8_e4m3fn, 7), "e5m2": (ml_dtypes.float8_e5m2, 14)}[fmt]
    v = np.moveaxis(np.asarray(x, np.float32).astype(ml_dtypes.bfloat16).astype(np.float64), axis, -1)
    blocks = v.reshape(v.shape[:-1] + (-1, 32))
    amax = np.abs(blocks).max(-1, keepdims=True)
    byte = np.maximum(np.where(amax > 0, np.frexp(amax)[1] - 1 + 127, 0) - down, 1)
    scale = np.exp2(byte - 127.0)
    codes = (blocks / scale).astype(np.float32).astype(dtype).astype(np.float64)
    return np.moveaxis((codes * scale).reshape(v.shape), -1, axis)


WIDE = False


def mx_kscale(k):
    if not WIDE:
        return np.ones(k)
    levels = np.array([10, -10, 5, -5, 0])
    if k % 512:
        return np.exp2(np.random.permutation(np.resize(levels, k // 32))).repeat(32)
    a = np.empty((k // 512, 16))
    for p in range(k // 512):
        a[p, :8] = np.random.permutation(np.resize(levels, 8))
        for g in range(8):
            far = levels[np.abs(levels - a[p, g]) >= 10]
            a[p, g + 8] = far[np.random.randint(len(far))]
    return np.exp2(a.ravel()).repeat(32)


BF16 = ml_dtypes.bfloat16


def bf(x):
    return np.asarray(x, np.float32).astype(BF16)


def f64(x):
    return np.asarray(x).astype(np.float64)


E2M1 = np.array([0.0, 0.5, 1.0, 1.5, 2.0, 3.0, 4.0, 6.0, -0.0, -0.5, -1.0, -1.5, -2.0, -3.0, -4.0, -6.0])


def pack_weight(w, fmt):
    k, n = w.shape
    w = f64(bf(w)).reshape(k // 32, 32, n)
    amax = np.abs(w).max(1)
    if fmt == "e4m3":
        byte = np.frexp(amax)[1] - 1 + 127 - 7
    else:
        mant, ex = np.frexp(amax / 6.0)
        byte = np.where(mant > 0.5, ex, ex - 1) + 127
    byte = np.clip(np.where(amax > 0, byte, 1), 1, 254)
    scaled = (w * np.exp2(127.0 - byte)[:, None, :]).reshape(k, n).astype(np.float32)
    by_word = np.ascontiguousarray(scaled.reshape(k // 512, 128, 4, n).transpose(0, 1, 3, 2))
    if fmt == "e4m3":
        words = by_word.astype(ml_dtypes.float8_e4m3fn).view(np.uint8)
    else:
        c = by_word.astype(ml_dtypes.float4_e2m1fn).view(np.uint8) & 0xF
        words = c[..., 0::2] | (c[..., 1::2] << 4)
    return np.ascontiguousarray(words), np.ascontiguousarray(byte.astype(np.uint8).reshape(k // 512, 16, n))


def unpack_weight(words, scales, fmt):
    g, p, n, _ = words.shape
    if fmt == "e4m3":
        vals = np.ascontiguousarray(words).view(ml_dtypes.float8_e4m3fn).astype(np.float64)
    else:
        nib = np.empty((g, p, n, 4), np.uint8)
        nib[..., 0::2] = words & 0xF
        nib[..., 1::2] = words >> 4
        vals = E2M1[nib]
    vals = vals * np.repeat(np.exp2(scales.astype(np.float64) - 127.0), 8, axis=1)[..., None]
    return vals.transpose(0, 1, 3, 2).reshape(g * 512, n)
def pack4(w):
    words, scales = pack_weight(w, "e2m1")
    return words.reshape(words.shape[0], 128, -1), scales


def unpack4(words, scales):
    return unpack_weight(words.reshape(words.shape[0], 128, -1, 2), scales, "e2m1")


E4M3FN = np.array([(-1.0 if i & 128 else 1.0) * ((1.0 + (i & 7) / 8.0) * 2.0 ** (((i >> 3) & 15) - 7) if i & 120 else (i & 7) * 2.0 ** -9) for i in range(256)])


def e4m3fn_bytes(y):
    return np.clip(np.asarray(y, np.float64), -448.0, 448.0).astype(np.float32).astype(ml_dtypes.float8_e4m3fn).view(np.uint8)


def e4m3fn_values(b):
    return E4M3FN[b]

def planes(Y):
    n, m = Y.shape
    b = f64(bf(Y)).reshape(n // 32, 32, m)
    amax = np.abs(b).max(1)
    byte = np.clip(np.where(amax > 0, np.frexp(amax)[1] - 1 + 127 - 7, 1), 1, 254)
    codes = (b * np.exp2(127.0 - byte)[:, None, :]).reshape(n, m).astype(np.float32).astype(ml_dtypes.float8_e4m3fn).view(np.uint8)
    words = codes.reshape(n // 512, 128, 4, m).transpose(0, 1, 3, 2)
    return np.ascontiguousarray(words), np.ascontiguousarray(byte.astype(np.uint8).reshape(n // 512, 16, m))


T, D, F, N, B = 1536, 1024, 1536, 1024, 128


def setup_inputs():
    s = mx_kscale(D)
    t = mx_kscale(F)
    X = np.random.randn(D, T)
    R = 0.6 * np.random.randn(D, F) / np.sqrt(D)
    x_words, x_scales = pack4(X * s[:, None])
    r_words, r_scales = pack4(R / s[:, None])
    base = np.exp(0.3 * np.random.randn(1, F)) * t[None, :]
    C = 0.8 * np.random.randn(F, N) / np.sqrt(F) / t[:, None]
    C_scale = (np.abs(C).reshape(F // B, B, N // B, B).max(axis=(1, 3)) / 448.0).astype(np.float32)
    C_bytes = e4m3fn_bytes(C / f64(np.repeat(np.repeat(C_scale, B, axis=0), B, axis=1)))
    bias = 0.4 * np.random.randn(1, N)
    amp = np.exp(0.8 * np.random.randn(1, N))
    return {"x_words": x_words, "x_scales": x_scales, "r_words": r_words, "r_scales": r_scales,
            "C_bytes": C_bytes, "C_scale": C_scale, "base": bf(base), "bias": bf(bias), "amp": bf(amp)}


def reference(x_words, x_scales, r_words, r_scales, C_bytes, C_scale, base, bias, amp):
    X = unpack4(x_words, x_scales)
    R = unpack4(r_words, r_scales)
    C = e4m3fn_values(C_bytes) * np.repeat(np.repeat(f64(C_scale), B, axis=0), B, axis=1)
    U = X.T @ R
    H = np.exp(U) * f64(base)
    Z = mxq(H, 1, "e4m3") @ mxq(C, 0, "e4m3")
    y = np.log1p(np.exp(Z + f64(bias))) * f64(amp)
    words, scales = planes(y.T)
    return y, words, scales

@@ -1,0 +1,360 @@
+from contextlib import ExitStack
+
+import concourse.mybir as mybir
+from concourse.masks import make_identity
+
+T, D, F, N = 1536, 1024, 1536, 1024
+FLOPS = 2 * T * D * F + 2 * T * F * N
+
+F32 = mybir.dt.float32
+BF16 = mybir.dt.bfloat16
+I32 = mybir.dt.int32
+U32 = mybir.dt.uint32
+U8 = mybir.dt.uint8
+FP8 = mybir.dt.float8_e4m3fn
+FP8X4 = mybir.dt.float8_e4m3fn_x4
+FP4X4 = mybir.dt.float4_e2m1fn_x4
+ACT = mybir.ActivationFunctionType
+ALU = mybir.AluOpType
+
+P = 128
+PACK = 4
+PASS = P * PACK
+CHUNK = 512
+D_PASSES = D // PASS
+F_PASSES = F // PASS
+N_GROUPS = N // PASS
+CHUNKS = T // CHUNK
+MM_BANKS = 5
+LN_EDGE = 2.0 ** 63
+
+
+def tile_spike_rate_coupling_b16_kernel(
+    tc, x_words, x_scales, r_words, r_scales, C_bytes, C_scale, base, bias, amp, out_0, out_1, out_2
+):
+    nc = tc.nc
+    with ExitStack() as ctx:
+        keep = ctx.enter_context(tc.tile_pool(name="keep", bufs=1))
+        work = ctx.enter_context(tc.tile_pool(name="work", bufs=2))
+        psum = ctx.enter_context(tc.psum_pool(name="psum", bufs=8))
+        ctx.enter_context(tc.manual_schedule())
+
+        def kept(name, shape, dtype):
+            return keep.tile(shape, dtype, name=name, align_bytes=64)
+
+        x_scale_plane = kept("x_scale_plane", [P, D_PASSES, T], U8)
+        r_scale_raw = kept("r_scale_raw", [P, D_PASSES, F], U8)
+        x_code = [kept("x_code%d" % c, [P, D_PASSES, 2 * CHUNK], U8) for c in range(CHUNKS)]
+        r_raw = [kept("r_raw%d" % g, [P, D_PASSES, 2 * PASS], U8) for g in range(F_PASSES)]
+        r_code = [kept("r_code%d" % g, [P, D_PASSES, 2 * PASS], U8) for g in range(F_PASSES)]
+        r_scale = [kept("r_scale%d" % g, [P, D_PASSES, PASS], U8) for g in range(F_PASSES)]
+        c_fp8 = [kept("c_fp8_%d" % g, [P, PACK, N], U8) for g in range(F_PASSES)]
+        c_code = {(g, n): kept("c_code%d_%d" % (g, n), [P, PASS], U32) for g in range(F_PASSES) for n in range(N_GROUPS)}
+        c_plane = {k: kept("c_plane%d_%d" % k, [P, PASS], U8) for k in c_code}
+        h_code = {(g, c): kept("h_code%d_%d" % (g, c), [P, CHUNK], U32) for g in range(F_PASSES) for c in range(CHUNKS)}
+        h_plane = {k: kept("h_plane%d_%d" % k, [P, CHUNK], U8) for k in h_code}
+        rate = {(n, c): kept("rate%d_%d" % (n, c), [P, PACK, CHUNK], F32) for n in range(N_GROUPS) for c in range(CHUNKS)}
+        y_plane = kept("y_plane", [P, N_GROUPS, T], U8)
+        base_rows = kept("base_rows", [PACK, F // PACK], BF16)
+        base_wide = kept("base_wide", [P, F // PACK], F32)
+        base_parts = kept("base_parts", [P, 3, F_PASSES * PACK], F32)
+        ln_base = kept("ln_base", [P, F_PASSES * PACK], F32)
+        bias_col = kept("bias_col", [P, N_GROUPS, PACK], BF16)
+        amp_col = kept("amp_col", [P, N_GROUPS, PACK], BF16)
+        c_scale_all = kept("c_scale_all", [P, F // P, N // P], F32)
+        c_scale_col = kept("c_scale_col", [P, F_PASSES, N // P], F32)
+        identity = kept("identity", [P, P], F32)
+        h_rows, h_words, c_wide, c_words, y_words, y_out = {}, {}, {}, {}, {}, {}
+
+        def load_words(dst, words, i):
+            src = words[:, :, 2 * PASS * i : 2 * PASS * (i + 1)].rearrange("d p n -> p d n")
+            nc.sync.dma_start(out=dst[:].bitcast(I32), in_=src.bitcast(I32))
+
+        def load_scale_rows(dst, rows):
+            for q in range(4):
+                src = rows[:, 4 * q : 4 * q + 4, :].rearrange("d r n -> r d n")
+                nc.sync.dma_start(out=dst[32 * q : 32 * q + 4, :, :].bitcast(I32), in_=src.bitcast(I32))
+
+        def load_columns(dst, vec):
+            nc.sync.dma_start(out=dst[:], in_=vec.rearrange("o (g p t) -> p (o g) t", p=P, t=PACK))
+
+        def load_c(g):
+            src = C_bytes[PASS * g : PASS * (g + 1), :].rearrange("(q t r) n -> t q r n", t=PACK, r=8)
+            for t in range(PACK):
+                nc.sync.dma_start(out=c_fp8[g][:, t, :], in_=src[t])
+
+        def sort_r_scales(g):
+            nc.vector.tensor_copy(
+                out=r_scale[g][:].bitcast(I32).rearrange("p d (t q w) -> p d t q w", t=PACK, w=2),
+                in_=r_scale_raw[:, :, PASS * g : PASS * (g + 1)].bitcast(I32).rearrange("p d (q t w) -> p d t q w", t=PACK, w=2),
+            )
+
+        def sort_r_codes(g):
+            nc.vector.tensor_copy(
+                out=r_code[g][:].bitcast(I32).rearrange("p d (t q w) -> p d t q w", t=PACK, w=4),
+                in_=r_raw[g][:].bitcast(I32).rearrange("p d (q t w) -> p d t q w", t=PACK, w=4),
+            )
+
+        def drive(g, c):
+            rows = work.tile([P, PACK, CHUNK], BF16, name="h_rows", bufs=6, align_bytes=64)
+            h_rows[g, c] = rows
+            for t in range(PACK):
+                bank = psum.tile([P, CHUNK], F32, name="bank", bufs=MM_BANKS)
+                for d in range(D_PASSES):
+                    nc.tensor.matmul_mx(
+                        out=bank[:],
+                        lhsT=r_code[g][:, d, 2 * P * t : 2 * P * (t + 1)].bitcast(FP4X4),
+                        lhsT_scale=r_scale[g][:, d, P * t : P * (t + 1)],
+                        rhs=x_code[c][:, d, :].bitcast(FP4X4),
+                        rhs_scale=x_scale_plane[:, d, CHUNK * c : CHUNK * (c + 1)],
+                        start=(d == 0),
+                        stop=(d == D_PASSES - 1),
+                    )
+                col = PACK * g + t
+                nc.scalar.activation(out=rows[:, t, :], in_=bank[:], func=ACT.Exp, bias=ln_base[:, col : col + 1])
+
+        def interleave(dst, rows):
+            nc.vector.tensor_copy(
+                out=dst[:].rearrange("p (a i t) -> p a t i", i=4, t=PACK),
+                in_=rows[:].rearrange("p t (a i) -> p a t i", i=4),
+            )
+
+        def interleave_h(g, c):
+            words = work.tile([P, PACK * CHUNK], BF16, name="h_words", bufs=3, align_bytes=64)
+            h_words[g, c] = words
+            interleave(words, h_rows[g, c])
+
+        def quantize_h(g, c):
+            nc.vector.quantize_mx(out=h_code[g, c][:].bitcast(FP8X4), scales=h_plane[g, c][:], in_=h_words[g, c][:])
+
+        def widen_c(g, n, on_scalar):
+            wide = work.tile([P, PACK * PASS], BF16, name="c_wide", bufs=3, align_bytes=64)
+            c_wide[g, n] = wide
+            for t in range(PACK):
+                src = c_fp8[g][:, t, PASS * n : PASS * (n + 1)].bitcast(FP8)
+                dst = wide[:, PASS * t : PASS * (t + 1)]
+                if on_scalar:
+                    nc.scalar.copy(out=dst, in_=src)
+                else:
+                    nc.vector.tensor_copy(out=dst, in_=src)
+
+        def scale_c(g, n):
+            words = work.tile([P, PACK * PASS], BF16, name="c_words", align_bytes=64)
+            c_words[g, n] = words
+            dst = words[:].rearrange("p (t m j) -> p t m j", t=PACK, j=PACK)
+            src = c_wide[g, n][:].rearrange("p (j m t) -> p t m j", t=PACK, j=PACK)
+            for b in range(PASS // P):
+                col = (PASS // P) * n + b
+                nc.vector.tensor_scalar(
+                    out=dst[:, :, 32 * b : 32 * (b + 1), :],
+                    in0=src[:, :, 32 * b : 32 * (b + 1), :],
+                    scalar1=c_scale_col[:, g, col : col + 1],
+                    scalar2=None,
+                    op0=ALU.mult,
+                )
+
+        def quantize_c(g, n):
+            nc.vector.quantize_mx(out=c_code[g, n][:].bitcast(FP8X4), scales=c_plane[g, n][:], in_=c_words[g, n][:])
+
+        def couple(n, c, width):
+            for t0 in range(0, PACK, width):
+                couple_banks(n, c, range(t0, t0 + width))
+
+        def couple_banks(n, c, slices):
+            banks = {t: psum.tile([P, CHUNK], F32, name="bank", bufs=MM_BANKS) for t in slices}
+            for g in range(F_PASSES):
+                for t in slices:
+                    nc.tensor.matmul_mx(
+                        out=banks[t][:],
+                        lhsT=c_code[g, n][:, P * t : P * (t + 1)].bitcast(FP8X4),
+                        lhsT_scale=c_plane[g, n][:, P * t : P * (t + 1)],
+                        rhs=h_code[g, c][:].bitcast(FP8X4),
+                        rhs_scale=h_plane[g, c][:],
+                        start=(g == 0),
+                        stop=(g == F_PASSES - 1),
+                    )
+            for t in slices:
+                nc.scalar.activation(out=rate[n, c][:, t, :], in_=banks[t][:], func=ACT.Exp, bias=bias_col[:, n, t : t + 1])
+
+        def log1p(n, c):
+            flat = rate[n, c][:].rearrange("p t m -> p (t m)")
+            nc.scalar.activation(out=flat, in_=flat, func=ACT.Ln, bias=1.0)
+
+        def amplify(n, c):
+            for t in range(PACK):
+                rows = rate[n, c][:, t, :]
+                nc.vector.tensor_scalar(out=rows, in0=rows, scalar1=amp_col[:, n, t : t + 1], scalar2=None, op0=ALU.mult)
+
+        def interleave_y(n, c):
+            words = work.tile([P, PACK * CHUNK], BF16, name="y_words", align_bytes=64)
+            y_words[n, c] = words
+            interleave(words, rate[n, c])
+
+        def quantize_y(n, c):
+            code = work.tile([P, CHUNK], U32, name="y_code", bufs=3, align_bytes=64)
+            nc.vector.quantize_mx(
+                out=code[:].bitcast(FP8X4), scales=y_plane[:, n, CHUNK * c : CHUNK * (c + 1)], in_=y_words[n, c][:]
+            )
+            dst = out_1[n].rearrange("p m t -> p (m t)")[:, PACK * CHUNK * c : PACK * CHUNK * (c + 1)]
+            nc.sync.dma_start(out=dst.bitcast(I32), in_=code[:].bitcast(I32))
+
+        def turn(n, c, half, on_scalar):
+            rows = work.tile([P, 2, PASS], F32, name="y_out", bufs=6, align_bytes=64)
+            for b in range(2 * half, 2 * half + 2):
+                bank = psum.tile([P, CHUNK], F32, name="turned", bufs=8 - MM_BANKS)
+                for t in range(PACK):
+                    nc.tensor.transpose(bank[:, P * t : P * (t + 1)], rate[n, c][:, t, P * b : P * (b + 1)], identity[:])
+                dst = rows[:, b % 2, :].rearrange("p (q t) -> p q t", t=PACK)
+                src = bank[:].rearrange("p (t q) -> p q t", t=PACK)
+                if on_scalar:
+                    nc.scalar.copy(out=dst, in_=src)
+                else:
+                    nc.vector.tensor_copy(out=dst, in_=src)
+                if b % 2 == 1:
+                    lo = CHUNK * c + P * (b - 1)
+                    dram = out_0[lo : lo + 2 * P, PASS * n : PASS * (n + 1)]
+                    nc.sync.dma_start(out=dram.rearrange("(b p) n -> p b n", p=P), in_=rows[:])
+
+        def store_y_plane(n):
+            for q in range(4):
+                nc.sync.dma_start(
+                    out=out_2[n, 4 * q : 4 * q + 4, :].bitcast(I32), in_=y_plane[32 * q : 32 * q + 4, n, :].bitcast(I32)
+                )
+
+        def split_base():
+            nc.vector.tensor_copy(out=base_wide[0:PACK, :], in_=base_rows[:])
+            bank = psum.tile([P, CHUNK], F32, name="turned", bufs=8 - MM_BANKS)
+            for g in range(F_PASSES):
+                nc.tensor.transpose(bank[:, P * g : P * (g + 1)], base_wide[:, P * g : P * (g + 1)], identity[:])
+            cols = bank[:, 0 : F_PASSES * P].rearrange("p (g t) -> p g t", g=F_PASSES)[:, :, 0:PACK]
+            for i, (s1, op0, s2, op1) in enumerate(
+                (
+                    (1.0 / LN_EDGE, ALU.max, LN_EDGE, ALU.min),
+                    (1.0 / LN_EDGE, ALU.mult, 1.0, ALU.max),
+                    (1.0 / LN_EDGE, ALU.min, LN_EDGE, ALU.mult),
+                )
+            ):
+                dst = base_parts[:, i, :].rearrange("p (g t) -> p g t", t=PACK)
+                nc.vector.tensor_scalar(out=dst, in0=cols, scalar1=s1, scalar2=s2, op0=op0, op1=op1)
+            parts = base_parts[:].rearrange("p i j -> p (i j)")
+            nc.scalar.activation(out=parts, in_=parts, func=ACT.Ln)
+
+        def sum_ln_base():
+            nc.vector.tensor_reduce(
+                out=ln_base[:], in_=base_parts[:].rearrange("p i j -> p j i"), axis=mybir.AxisListType.X, op=ALU.add
+            )
+
+        def pick_c_scales():
+            by_quadrant = c_scale_all[:].rearrange("p (g q) b -> p q g b", q=4)
+            for q in range(4):
+                rows = slice(32 * q, 32 * (q + 1))
+                nc.vector.tensor_copy(out=c_scale_col[rows, :, :], in_=by_quadrant[rows, q, :, :])
+
+        nc.vector.memset(r_scale_raw[:].bitcast(I32), 0)
+        nc.vector.memset(x_scale_plane[:].bitcast(I32), 0)
+        nc.vector.memset(base_wide[:], 0.0)
+        make_identity(nc, identity[:])
+        nc.sync.dma_start(
+            out=base_rows[:].rearrange("t (a r) -> t a r", r=8), in_=base.rearrange("o (a t r) -> t (o a) r", t=PACK, r=8)
+        )
+        load_words(r_raw[0], r_words, 0)
+        load_scale_rows(r_scale_raw, r_scales)
+        load_words(x_code[0], x_words, 0)
+        load_scale_rows(x_scale_plane, x_scales)
+        nc.sync.dma_start(
+            out=c_scale_all[:].rearrange("p i j -> p (i j)"), in_=C_scale.rearrange("i j -> (i j)").partition_broadcast(P)
+        )
+        load_c(0)
+        load_words(r_raw[1], r_words, 1)
+        load_words(r_raw[2], r_words, 2)
+        load_c(1)
+        load_words(x_code[1], x_words, 1)
+        load_c(2)
+        load_words(x_code[2], x_words, 2)
+        load_columns(bias_col, bias)
+        load_columns(amp_col, amp)
+
+        split_base()
+        sort_r_codes(0)
+        sort_r_scales(0)
+        sum_ln_base()
+        sort_r_scales(1)
+        sort_r_scales(2)
+        pick_c_scales()
+        drive(0, 0)
+        widen_c(0, 0, False)
+        sort_r_codes(1)
+        drive(1, 0)
+        for g in range(F_PASSES):
+            scale_c(g, 0)
+            if g == 0:
+                sort_r_codes(2)
+                drive(2, 0)
+            drive(g, 1)
+            interleave_h(g, 0)
+            quantize_c(g, 0)
+            if g + 1 < F_PASSES:
+                widen_c(g + 1, 0, False)
+            else:
+                interleave_h(0, 1)
+            quantize_h(g, 0)
+        for g in range(F_PASSES):
+            drive(g, 2)
+        couple(0, 0, 1)
+        widen_c(0, 1, True)
+        later = [(g, c) for c in range(1, CHUNKS) for g in range(F_PASSES)]
+        for i in range(len(later)):
+            if i + 1 < len(later):
+                interleave_h(*later[i + 1])
+            else:
+                scale_c(0, 1)
+            quantize_h(*later[i])
+            if later[i] == (F_PASSES - 1, 1):
+                couple(0, 1, PACK)
+        couple(0, 2, PACK)
+        widen_c(1, 1, False)
+        widen_c(2, 1, False)
+        quantize_c(0, 1)
+        scale_c(1, 1)
+        scale_c(2, 1)
+        quantize_c(1, 1)
+        for c in range(CHUNKS):
+            log1p(0, c)
+        quantize_c(2, 1)
+        amplify(0, 0)
+        couple(1, 0, 1)
+        amplify(0, 1)
+        interleave_y(0, 0)
+        turn(0, 0, 0, False)
+        turn(0, 0, 1, False)
+        couple(1, 1, 1)
+        couple(1, 2, 1)
+        amplify(0, 2)
+        interleave_y(0, 1)
+        quantize_y(0, 0)
+        interleave_y(0, 2)
+        quantize_y(0, 1)
+        for c in range(CHUNKS):
+            log1p(1, c)
+        turn(0, 1, 0, False)
+        quantize_y(0, 2)
+        store_y_plane(0)
+        turn(0, 1, 1, False)
+        turn(0, 2, 0, False)
+        amplify(1, 0)
+        turn(0, 2, 1, False)
+        amplify(1, 1)
+        turn(1, 0, 0, True)
+        turn(1, 0, 1, True)
+        interleave_y(1, 0)
+        amplify(1, 2)
+        turn(1, 1, 0, True)
+        quantize_y(1, 0)
+        turn(1, 1, 1, True)
+        interleave_y(1, 1)
+        interleave_y(1, 2)
+        quantize_y(1, 1)
+        turn(1, 2, 0, True)
+        quantize_y(1, 2)
+        turn(1, 2, 1, True)
+        store_y_plane(1)

@@ -113,16 +113,16 @@ def tile_spike_rate_coupling_b16_kernel(
                 col = PACK * g + t
                 nc.scalar.activation(out=rows[:, t, :], in_=bank[:], func=ACT.Exp, bias=ln_base[:, col : col + 1])
 
-        def interleave(dst, rows):
+        def interleave(dst, rows, run):
             nc.vector.tensor_copy(
-                out=dst[:].rearrange("p (a i t) -> p a t i", i=4, t=PACK),
-                in_=rows[:].rearrange("p t (a i) -> p a t i", i=4),
+                out=dst[:].rearrange("p (a i t) -> p a t i", i=run, t=PACK),
+                in_=rows[:].rearrange("p t (a i) -> p a t i", i=run),
             )
 
         def interleave_h(g, c):
             words = work.tile([P, PACK * CHUNK], BF16, name="h_words", bufs=3, align_bytes=64)
             h_words[g, c] = words
-            interleave(words, h_rows[g, c])
+            interleave(words, h_rows[g, c], 4)
 
         def quantize_h(g, c):
             nc.vector.quantize_mx(out=h_code[g, c][:].bitcast(FP8X4), scales=h_plane[g, c][:], in_=h_words[g, c][:])
@@ -139,15 +139,15 @@ def tile_spike_rate_coupling_b16_kernel(
                     nc.vector.tensor_copy(out=dst, in_=src)
 
         def scale_c(g, n):
-            words = work.tile([P, PACK * PASS], BF16, name="c_words", align_bytes=64)
+            words = work.tile([P, PACK * PASS], BF16, name="c_words", bufs=3, align_bytes=64)
             c_words[g, n] = words
-            dst = words[:].rearrange("p (t m j) -> p t m j", t=PACK, j=PACK)
-            src = c_wide[g, n][:].rearrange("p (j m t) -> p t m j", t=PACK, j=PACK)
+            dst = words[:].rearrange("p (t m j) -> p m j t", t=PACK, j=PACK)
+            src = c_wide[g, n][:].rearrange("p (j m t) -> p m j t", t=PACK, j=PACK)
             for b in range(PASS // P):
                 col = (PASS // P) * n + b
                 nc.vector.tensor_scalar(
-                    out=dst[:, :, 32 * b : 32 * (b + 1), :],
-                    in0=src[:, :, 32 * b : 32 * (b + 1), :],
+                    out=dst[:, 32 * b : 32 * (b + 1), :, :],
+                    in0=src[:, 32 * b : 32 * (b + 1), :, :],
                     scalar1=c_scale_col[:, g, col : col + 1],
                     scalar2=None,
                     op0=ALU.mult,
@@ -188,7 +188,7 @@ def tile_spike_rate_coupling_b16_kernel(
         def interleave_y(n, c):
             words = work.tile([P, PACK * CHUNK], BF16, name="y_words", align_bytes=64)
             y_words[n, c] = words
-            interleave(words, rate[n, c])
+            interleave(words, rate[n, c], 4)
 
         def quantize_y(n, c):
             code = work.tile([P, CHUNK], U32, name="y_code", bufs=3, align_bytes=64)
@@ -201,7 +201,10 @@ def tile_spike_rate_coupling_b16_kernel(
         def turn(n, c, half, on_scalar):
             rows = work.tile([P, 2, PASS], F32, name="y_out", bufs=6, align_bytes=64)
             for b in range(2 * half, 2 * half + 2):
-                bank = psum.tile([P, CHUNK], F32, name="turned", bufs=8 - MM_BANKS)
+                if n == N_GROUPS - 1:
+                    bank = psum.tile([P, CHUNK], F32, name="bank", bufs=MM_BANKS)
+                else:
+                    bank = psum.tile([P, CHUNK], F32, name="turned", bufs=8 - MM_BANKS)
                 for t in range(PACK):
                     nc.tensor.transpose(bank[:, P * t : P * (t + 1)], rate[n, c][:, t, P * b : P * (b + 1)], identity[:])
                 dst = rows[:, b % 2, :].rearrange("p (q t) -> p q t", t=PACK)
@@ -280,81 +283,90 @@ def tile_spike_rate_coupling_b16_kernel(
         sum_ln_base()
         sort_r_scales(1)
         sort_r_scales(2)
-        pick_c_scales()
         drive(0, 0)
         widen_c(0, 0, False)
+        pick_c_scales()
         sort_r_codes(1)
         drive(1, 0)
+        W = [0,1,1,0]
         for g in range(F_PASSES):
             scale_c(g, 0)
             if g == 0:
                 sort_r_codes(2)
                 drive(2, 0)
+            if g == 1 and W[0]:
+                widen_c(2, 0, True)
             drive(g, 1)
             interleave_h(g, 0)
             quantize_c(g, 0)
             if g + 1 < F_PASSES:
-                widen_c(g + 1, 0, False)
+                if not (g == 1 and W[0]):
+                    widen_c(g + 1, 0, False)
             else:
                 interleave_h(0, 1)
             quantize_h(g, 0)
         for g in range(F_PASSES):
             drive(g, 2)
-        couple(0, 0, 1)
         widen_c(0, 1, True)
+        couple(0, 0, 1)
         later = [(g, c) for c in range(1, CHUNKS) for g in range(F_PASSES)]
         for i in range(len(later)):
             if i + 1 < len(later):
                 interleave_h(*later[i + 1])
-            else:
-                scale_c(0, 1)
             quantize_h(*later[i])
             if later[i] == (F_PASSES - 1, 1):
-                couple(0, 1, PACK)
+                couple(0, 1, W[2])
+                if W[1]:
+                    widen_c(1, 1, True)
         couple(0, 2, PACK)
-        widen_c(1, 1, False)
+        scale_c(0, 1)
+        if not W[1]:
+            widen_c(1, 1, False)
         widen_c(2, 1, False)
-        quantize_c(0, 1)
         scale_c(1, 1)
+        quantize_c(0, 1)
         scale_c(2, 1)
         quantize_c(1, 1)
         for c in range(CHUNKS):
             log1p(0, c)
         quantize_c(2, 1)
-        amplify(0, 0)
         couple(1, 0, 1)
+        couple_banks(1, 1, range(0, 1))
+        amplify(0, 0)
         amplify(0, 1)
         interleave_y(0, 0)
-        turn(0, 0, 0, False)
-        turn(0, 0, 1, False)
-        couple(1, 1, 1)
-        couple(1, 2, 1)
         amplify(0, 2)
-        interleave_y(0, 1)
+        turn(0, 0, 0, False)
+        for t in range(1, PACK):
+            couple_banks(1, 1, range(t, t + 1))
         quantize_y(0, 0)
+        interleave_y(0, 1)
+        couple(1, 2, 1)
         interleave_y(0, 2)
         quantize_y(0, 1)
-        for c in range(CHUNKS):
-            log1p(1, c)
-        turn(0, 1, 0, False)
+        log1p(1, 0)
+        log1p(1, 1)
         quantize_y(0, 2)
+        turn(0, 0, 1, False)
         store_y_plane(0)
+        turn(0, 1, 0, False)
         turn(0, 1, 1, False)
         turn(0, 2, 0, False)
         amplify(1, 0)
-        turn(0, 2, 1, False)
         amplify(1, 1)
         turn(1, 0, 0, True)
         turn(1, 0, 1, True)
+        log1p(1, 2)
+        turn(0, 2, 1, False)
         interleave_y(1, 0)
-        amplify(1, 2)
         turn(1, 1, 0, True)
+        amplify(1, 2)
         quantize_y(1, 0)
         turn(1, 1, 1, True)
         interleave_y(1, 1)
+        turn(1, 2, 0, True)
         interleave_y(1, 2)
         quantize_y(1, 1)
-        turn(1, 2, 0, True)
-        quantize_y(1, 2)
         turn(1, 2, 1, True)
+        quantize_y(1, 2)
         store_y_plane(1)

from contextlib import ExitStack

import concourse.mybir as mybir
from concourse.masks import make_identity

T, D, F, N = 1536, 1024, 1536, 1024
FLOPS = 2 * T * D * F + 2 * T * F * N

F32 = mybir.dt.float32
BF16 = mybir.dt.bfloat16
I32 = mybir.dt.int32
U32 = mybir.dt.uint32
U8 = mybir.dt.uint8
FP8 = mybir.dt.float8_e4m3fn
FP8X4 = mybir.dt.float8_e4m3fn_x4
FP4X4 = mybir.dt.float4_e2m1fn_x4
ACT = mybir.ActivationFunctionType
ALU = mybir.AluOpType

P = 128
PACK = 4
PASS = P * PACK
CHUNK = 512
D_PASSES = D // PASS
F_PASSES = F // PASS
N_GROUPS = N // PASS
CHUNKS = T // CHUNK
MM_BANKS = 5
LN_EDGE = 2.0 ** 63


def tile_spike_rate_coupling_b16_kernel(
    tc, x_words, x_scales, r_words, r_scales, C_bytes, C_scale, base, bias, amp, out_0, out_1, out_2
):
    nc = tc.nc
    with ExitStack() as ctx:
        keep = ctx.enter_context(tc.tile_pool(name="keep", bufs=1))
        work = ctx.enter_context(tc.tile_pool(name="work", bufs=2))
        psum = ctx.enter_context(tc.psum_pool(name="psum", bufs=8))
        ctx.enter_context(tc.manual_schedule())

        def kept(name, shape, dtype):
            return keep.tile(shape, dtype, name=name, align_bytes=64)

        x_scale_plane = kept("x_scale_plane", [P, D_PASSES, T], U8)
        r_scale_raw = kept("r_scale_raw", [P, D_PASSES, F], U8)
        x_code = [kept("x_code%d" % c, [P, D_PASSES, 2 * CHUNK], U8) for c in range(CHUNKS)]
        r_raw = [kept("r_raw%d" % g, [P, D_PASSES, 2 * PASS], U8) for g in range(F_PASSES)]
        r_code = [kept("r_code%d" % g, [P, D_PASSES, 2 * PASS], U8) for g in range(F_PASSES)]
        r_scale = [kept("r_scale%d" % g, [P, D_PASSES, PASS], U8) for g in range(F_PASSES)]
        c_fp8 = [kept("c_fp8_%d" % g, [P, PACK, N], U8) for g in range(F_PASSES)]
        c_code = {(g, n): kept("c_code%d_%d" % (g, n), [P, PASS], U32) for g in range(F_PASSES) for n in range(N_GROUPS)}
        c_plane = {k: kept("c_plane%d_%d" % k, [P, PASS], U8) for k in c_code}
        h_code = {(g, c): kept("h_code%d_%d" % (g, c), [P, CHUNK], U32) for g in range(F_PASSES) for c in range(CHUNKS)}
        h_plane = {k: kept("h_plane%d_%d" % k, [P, CHUNK], U8) for k in h_code}
        rate = {(n, c): kept("rate%d_%d" % (n, c), [P, PACK, CHUNK], F32) for n in range(N_GROUPS) for c in range(CHUNKS)}
        y_plane = kept("y_plane", [P, N_GROUPS, T], U8)
        base_rows = kept("base_rows", [PACK, F // PACK], BF16)
        base_wide = kept("base_wide", [P, F // PACK], F32)
        base_parts = kept("base_parts", [P, 3, F_PASSES * PACK], F32)
        ln_base = kept("ln_base", [P, F_PASSES * PACK], F32)
        bias_col = kept("bias_col", [P, N_GROUPS, PACK], BF16)
        amp_col = kept("amp_col", [P, N_GROUPS, PACK], BF16)
        c_scale_all = kept("c_scale_all", [P, F // P, N // P], F32)
        c_scale_col = kept("c_scale_col", [P, F_PASSES, N // P], F32)
        identity = kept("identity", [P, P], F32)
        h_rows, h_words, c_wide, c_words, y_words, y_out = {}, {}, {}, {}, {}, {}

        def load_words(dst, words, i):
            src = words[:, :, 2 * PASS * i : 2 * PASS * (i + 1)].rearrange("d p n -> p d n")
            nc.sync.dma_start(out=dst[:].bitcast(I32), in_=src.bitcast(I32))

        def load_scale_rows(dst, rows):
            for q in range(4):
                src = rows[:, 4 * q : 4 * q + 4, :].rearrange("d r n -> r d n")
                nc.sync.dma_start(out=dst[32 * q : 32 * q + 4, :, :].bitcast(I32), in_=src.bitcast(I32))

        def load_columns(dst, vec):
            nc.sync.dma_start(out=dst[:], in_=vec.rearrange("o (g p t) -> p (o g) t", p=P, t=PACK))

        def load_c(g):
            src = C_bytes[PASS * g : PASS * (g + 1), :].rearrange("(q t r) n -> t q r n", t=PACK, r=8)
            for t in range(PACK):
                nc.sync.dma_start(out=c_fp8[g][:, t, :], in_=src[t])

        def sort_r_scales(g):
            nc.vector.tensor_copy(
                out=r_scale[g][:].bitcast(I32).rearrange("p d (t q w) -> p d t q w", t=PACK, w=2),
                in_=r_scale_raw[:, :, PASS * g : PASS * (g + 1)].bitcast(I32).rearrange("p d (q t w) -> p d t q w", t=PACK, w=2),
            )

        def sort_r_codes(g):
            nc.vector.tensor_copy(
                out=r_code[g][:].bitcast(I32).rearrange("p d (t q w) -> p d t q w", t=PACK, w=4),
                in_=r_raw[g][:].bitcast(I32).rearrange("p d (q t w) -> p d t q w", t=PACK, w=4),
            )

        def drive(g, c):
            rows = work.tile([P, PACK, CHUNK], BF16, name="h_rows", bufs=6, align_bytes=64)
            h_rows[g, c] = rows
            for t in range(PACK):
                bank = psum.tile([P, CHUNK], F32, name="bank", bufs=MM_BANKS)
                for d in range(D_PASSES):
                    nc.tensor.matmul_mx(
                        out=bank[:],
                        lhsT=r_code[g][:, d, 2 * P * t : 2 * P * (t + 1)].bitcast(FP4X4),
                        lhsT_scale=r_scale[g][:, d, P * t : P * (t + 1)],
                        rhs=x_code[c][:, d, :].bitcast(FP4X4),
                        rhs_scale=x_scale_plane[:, d, CHUNK * c : CHUNK * (c + 1)],
                        start=(d == 0),
                        stop=(d == D_PASSES - 1),
                    )
                col = PACK * g + t
                nc.scalar.activation(out=rows[:, t, :], in_=bank[:], func=ACT.Exp, bias=ln_base[:, col : col + 1])

        def interleave(dst, rows, run):
            nc.vector.tensor_copy(
                out=dst[:].rearrange("p (a i t) -> p a t i", i=run, t=PACK),
                in_=rows[:].rearrange("p t (a i) -> p a t i", i=run),
            )

        def interleave_h(g, c):
            words = work.tile([P, PACK * CHUNK], BF16, name="h_words", bufs=3, align_bytes=64)
            h_words[g, c] = words
            interleave(words, h_rows[g, c], 4)

        def quantize_h(g, c):
            nc.vector.quantize_mx(out=h_code[g, c][:].bitcast(FP8X4), scales=h_plane[g, c][:], in_=h_words[g, c][:])

        def widen_c(g, n, on_scalar):
            wide = work.tile([P, PACK * PASS], BF16, name="c_wide", bufs=3, align_bytes=64)
            c_wide[g, n] = wide
            for t in range(PACK):
                src = c_fp8[g][:, t, PASS * n : PASS * (n + 1)].bitcast(FP8)
                dst = wide[:, PASS * t : PASS * (t + 1)]
                if on_scalar:
                    nc.scalar.copy(out=dst, in_=src)
                else:
                    nc.vector.tensor_copy(out=dst, in_=src)

        def scale_c(g, n):
            words = work.tile([P, PACK * PASS], BF16, name="c_words", bufs=3, align_bytes=64)
            c_words[g, n] = words
            dst = words[:].rearrange("p (t m j) -> p m j t", t=PACK, j=PACK)
            src = c_wide[g, n][:].rearrange("p (j m t) -> p m j t", t=PACK, j=PACK)
            for b in range(PASS // P):
                col = (PASS // P) * n + b
                nc.vector.tensor_scalar(
                    out=dst[:, 32 * b : 32 * (b + 1), :, :],
                    in0=src[:, 32 * b : 32 * (b + 1), :, :],
                    scalar1=c_scale_col[:, g, col : col + 1],
                    scalar2=None,
                    op0=ALU.mult,
                )

        def quantize_c(g, n):
            nc.vector.quantize_mx(out=c_code[g, n][:].bitcast(FP8X4), scales=c_plane[g, n][:], in_=c_words[g, n][:])

        def couple(n, c, width):
            for t0 in range(0, PACK, width):
                couple_banks(n, c, range(t0, t0 + width))

        def couple_banks(n, c, slices):
            banks = {t: psum.tile([P, CHUNK], F32, name="bank", bufs=MM_BANKS) for t in slices}
            for g in range(F_PASSES):
                for t in slices:
                    nc.tensor.matmul_mx(
                        out=banks[t][:],
                        lhsT=c_code[g, n][:, P * t : P * (t + 1)].bitcast(FP8X4),
                        lhsT_scale=c_plane[g, n][:, P * t : P * (t + 1)],
                        rhs=h_code[g, c][:].bitcast(FP8X4),
                        rhs_scale=h_plane[g, c][:],
                        start=(g == 0),
                        stop=(g == F_PASSES - 1),
                    )
            for t in slices:
                nc.scalar.activation(out=rate[n, c][:, t, :], in_=banks[t][:], func=ACT.Exp, bias=bias_col[:, n, t : t + 1])

        def log1p(n, c):
            flat = rate[n, c][:].rearrange("p t m -> p (t m)")
            nc.scalar.activation(out=flat, in_=flat, func=ACT.Ln, bias=1.0)

        def amplify(n, c):
            for t in range(PACK):
                rows = rate[n, c][:, t, :]
                nc.vector.tensor_scalar(out=rows, in0=rows, scalar1=amp_col[:, n, t : t + 1], scalar2=None, op0=ALU.mult)

        def interleave_y(n, c):
            words = work.tile([P, PACK * CHUNK], BF16, name="y_words", align_bytes=64)
            y_words[n, c] = words
            interleave(words, rate[n, c], 4)

        def quantize_y(n, c):
            code = work.tile([P, CHUNK], U32, name="y_code", bufs=3, align_bytes=64)
            nc.vector.quantize_mx(
                out=code[:].bitcast(FP8X4), scales=y_plane[:, n, CHUNK * c : CHUNK * (c + 1)], in_=y_words[n, c][:]
            )
            dst = out_1[n].rearrange("p m t -> p (m t)")[:, PACK * CHUNK * c : PACK * CHUNK * (c + 1)]
            nc.sync.dma_start(out=dst.bitcast(I32), in_=code[:].bitcast(I32))

        def turn(n, c, half, on_scalar):
            rows = work.tile([P, 2, PASS], F32, name="y_out", bufs=6, align_bytes=64)
            for b in range(2 * half, 2 * half + 2):
                if n == N_GROUPS - 1:
                    bank = psum.tile([P, CHUNK], F32, name="bank", bufs=MM_BANKS)
                else:
                    bank = psum.tile([P, CHUNK], F32, name="turned", bufs=8 - MM_BANKS)
                for t in range(PACK):
                    nc.tensor.transpose(bank[:, P * t : P * (t + 1)], rate[n, c][:, t, P * b : P * (b + 1)], identity[:])
                dst = rows[:, b % 2, :].rearrange("p (q t) -> p q t", t=PACK)
                src = bank[:].rearrange("p (t q) -> p q t", t=PACK)
                if on_scalar:
                    nc.scalar.copy(out=dst, in_=src)
                else:
                    nc.vector.tensor_copy(out=dst, in_=src)
                if b % 2 == 1:
                    lo = CHUNK * c + P * (b - 1)
                    dram = out_0[lo : lo + 2 * P, PASS * n : PASS * (n + 1)]
                    nc.sync.dma_start(out=dram.rearrange("(b p) n -> p b n", p=P), in_=rows[:])

        def store_y_plane(n):
            for q in range(4):
                nc.sync.dma_start(
                    out=out_2[n, 4 * q : 4 * q + 4, :].bitcast(I32), in_=y_plane[32 * q : 32 * q + 4, n, :].bitcast(I32)
                )

        def split_base():
            nc.vector.tensor_copy(out=base_wide[0:PACK, :], in_=base_rows[:])
            bank = psum.tile([P, CHUNK], F32, name="turned", bufs=8 - MM_BANKS)
            for g in range(F_PASSES):
                nc.tensor.transpose(bank[:, P * g : P * (g + 1)], base_wide[:, P * g : P * (g + 1)], identity[:])
            cols = bank[:, 0 : F_PASSES * P].rearrange("p (g t) -> p g t", g=F_PASSES)[:, :, 0:PACK]
            for i, (s1, op0, s2, op1) in enumerate(
                (
                    (1.0 / LN_EDGE, ALU.max, LN_EDGE, ALU.min),
                    (1.0 / LN_EDGE, ALU.mult, 1.0, ALU.max),
                    (1.0 / LN_EDGE, ALU.min, LN_EDGE, ALU.mult),
                )
            ):
                dst = base_parts[:, i, :].rearrange("p (g t) -> p g t", t=PACK)
                nc.vector.tensor_scalar(out=dst, in0=cols, scalar1=s1, scalar2=s2, op0=op0, op1=op1)
            parts = base_parts[:].rearrange("p i j -> p (i j)")
            nc.scalar.activation(out=parts, in_=parts, func=ACT.Ln)

        def sum_ln_base():
            nc.vector.tensor_reduce(
                out=ln_base[:], in_=base_parts[:].rearrange("p i j -> p j i"), axis=mybir.AxisListType.X, op=ALU.add
            )

        def pick_c_scales():
            by_quadrant = c_scale_all[:].rearrange("p (g q) b -> p q g b", q=4)
            for q in range(4):
                rows = slice(32 * q, 32 * (q + 1))
                nc.vector.tensor_copy(out=c_scale_col[rows, :, :], in_=by_quadrant[rows, q, :, :])

        nc.vector.memset(r_scale_raw[:].bitcast(I32), 0)
        nc.vector.memset(x_scale_plane[:].bitcast(I32), 0)
        nc.vector.memset(base_wide[:], 0.0)
        make_identity(nc, identity[:])
        nc.sync.dma_start(
            out=base_rows[:].rearrange("t (a r) -> t a r", r=8), in_=base.rearrange("o (a t r) -> t (o a) r", t=PACK, r=8)
        )
        load_words(r_raw[0], r_words, 0)
        load_scale_rows(r_scale_raw, r_scales)
        load_words(x_code[0], x_words, 0)
        load_scale_rows(x_scale_plane, x_scales)
        nc.sync.dma_start(
            out=c_scale_all[:].rearrange("p i j -> p (i j)"), in_=C_scale.rearrange("i j -> (i j)").partition_broadcast(P)
        )
        load_c(0)
        load_words(r_raw[1], r_words, 1)
        load_words(r_raw[2], r_words, 2)
        load_c(1)
        load_words(x_code[1], x_words, 1)
        load_c(2)
        load_words(x_code[2], x_words, 2)
        load_columns(bias_col, bias)
        load_columns(amp_col, amp)

        split_base()
        sort_r_codes(0)
        sort_r_scales(0)
        sum_ln_base()
        sort_r_scales(1)
        sort_r_scales(2)
        drive(0, 0)
        widen_c(0, 0, False)
        pick_c_scales()
        sort_r_codes(1)
        drive(1, 0)
        W = [0,1,1,0]
        for g in range(F_PASSES):
            scale_c(g, 0)
            if g == 0:
                sort_r_codes(2)
                drive(2, 0)
            if g == 1 and W[0]:
                widen_c(2, 0, True)
            drive(g, 1)
            interleave_h(g, 0)
            quantize_c(g, 0)
            if g + 1 < F_PASSES:
                if not (g == 1 and W[0]):
                    widen_c(g + 1, 0, False)
            else:
                interleave_h(0, 1)
            quantize_h(g, 0)
        for g in range(F_PASSES):
            drive(g, 2)
        widen_c(0, 1, True)
        couple(0, 0, 1)
        later = [(g, c) for c in range(1, CHUNKS) for g in range(F_PASSES)]
        for i in range(len(later)):
            if i + 1 < len(later):
                interleave_h(*later[i + 1])
            quantize_h(*later[i])
            if later[i] == (F_PASSES - 1, 1):
                couple(0, 1, W[2])
                if W[1]:
                    widen_c(1, 1, True)
        couple(0, 2, PACK)
        scale_c(0, 1)
        if not W[1]:
            widen_c(1, 1, False)
        widen_c(2, 1, False)
        scale_c(1, 1)
        quantize_c(0, 1)
        scale_c(2, 1)
        quantize_c(1, 1)
        for c in range(CHUNKS):
            log1p(0, c)
        quantize_c(2, 1)
        couple(1, 0, 1)
        couple_banks(1, 1, range(0, 1))
        amplify(0, 0)
        amplify(0, 1)
        interleave_y(0, 0)
        amplify(0, 2)
        turn(0, 0, 0, False)
        for t in range(1, PACK):
            couple_banks(1, 1, range(t, t + 1))
        quantize_y(0, 0)
        interleave_y(0, 1)
        couple(1, 2, 1)
        interleave_y(0, 2)
        quantize_y(0, 1)
        log1p(1, 0)
        log1p(1, 1)
        quantize_y(0, 2)
        turn(0, 0, 1, False)
        store_y_plane(0)
        turn(0, 1, 0, False)
        turn(0, 1, 1, False)
        turn(0, 2, 0, False)
        amplify(1, 0)
        amplify(1, 1)
        turn(1, 0, 0, True)
        turn(1, 0, 1, True)
        log1p(1, 2)
        turn(0, 2, 1, False)
        interleave_y(1, 0)
        turn(1, 1, 0, True)
        amplify(1, 2)
        quantize_y(1, 0)
        turn(1, 1, 1, True)
        interleave_y(1, 1)
        turn(1, 2, 0, True)
        interleave_y(1, 2)
        quantize_y(1, 1)
        turn(1, 2, 1, True)
        quantize_y(1, 2)
        store_y_plane(1)
